import numpy as np
CORES = [0,1,2,3,4,5,6,7,8,9,10,11,12,13,14,15,16,17,18,19,20,21,22,23,24,25,26,27,28,29,30,31,128,129,130,131,132,133,134,135,136,137,138,139,140,141,142,143,144,145,146,147,148,149,150,151,152,153,154,155,156,157,158,159]
N = 64
TOK, D = 32, 512
ROUTE = [[[1,32],[9,18],[41,45],[21,27],[33,36],[28,29],[6,52],[15,34],[19,22],[24,30],[49,54],[5,29],[29,54],[21,23],[46,60],[20,32],[5,7],[33,39],[40,55],[49,50],[28,30],[19,22],[58,60],[10,13],[40,62],[25,48],[4,11],[16,21],[26,28],[11,12],[6,7],[0,7]],[[29,31],[21,37],[9,13],[25,30],[50,51],[53,54],[26,27],[18,54],[27,34],[24,29],[28,38],[5,16],[50,51],[25,27],[16,17],[48,52],[6,48],[18,39],[49,54],[48,49],[4,6],[6,48],[48,53],[40,45],[28,29],[9,14],[29,50],[2,36],[12,13],[11,14],[48,54],[31,58]],[[6,25],[12,15],[43,60],[6,9],[25,29],[5,56],[3,6],[34,52],[35,39],[9,13],[26,54],[17,19],[12,56],[36,39],[33,34],[2,3],[48,53],[45,46],[0,12],[40,41],[4,7],[59,61],[11,13],[6,31],[5,55],[28,54],[17,60],[11,15],[21,22],[58,61],[59,60],[1,2]],[[9,10],[43,60],[59,61],[40,42],[56,57],[38,56],[5,42],[9,11],[8,9],[1,6],[58,61],[0,8],[11,55],[27,47],[48,50],[18,21],[50,51],[25,29],[8,11],[25,31],[2,24],[18,20],[62,63],[20,23],[1,40],[0,1],[0,3],[18,21],[40,44],[5,38],[48,49],[56,62]],[[40,42],[21,26],[47,61],[31,34],[15,60],[11,14],[52,55],[34,51],[17,23],[35,38],[61,62],[42,45],[33,37],[33,36],[0,2],[10,11],[5,25],[27,57],[28,31],[18,38],[17,30],[37,63],[51,52],[48,55],[19,20],[41,54],[32,37],[26,31],[5,56],[59,61],[3,26],[56,59]],[[4,57],[16,20],[54,55],[6,27],[28,31],[27,30],[56,63],[26,38],[8,59],[58,61],[8,28],[38,44],[36,52],[12,56],[28,34],[51,52],[40,49],[48,61],[48,50],[10,16],[37,38],[50,51],[3,52],[16,17],[0,7],[56,62],[43,53],[34,54],[20,22],[27,31],[15,46],[1,28]],[[9,10],[22,41],[48,51],[29,30],[10,49],[60,62],[49,54],[27,29],[0,1],[38,43],[22,27],[41,44],[12,13],[36,37],[22,30],[18,62],[12,14],[6,40],[33,47],[26,30],[42,45],[18,42],[59,60],[40,44],[15,47],[18,33],[23,27],[12,14],[49,55],[26,62],[35,37],[34,36]],[[29,57],[61,62],[38,39],[57,59],[14,15],[17,18],[22,23],[40,44],[48,51],[16,49],[22,23],[1,26],[13,45],[12,22],[6,37],[2,5],[0,2],[17,19],[60,61],[51,60],[2,6],[0,13],[8,14],[4,7],[4,6],[5,39],[3,11],[10,11],[52,55],[48,50],[9,12],[0,60]],[[16,62],[36,39],[45,47],[20,57],[21,29],[34,35],[0,3],[32,34],[13,15],[57,60],[9,14],[33,39],[41,42],[56,63],[13,14],[1,5],[51,53],[0,2],[34,38],[43,45],[32,39],[41,44],[37,39],[57,60],[45,47],[4,6],[58,59],[8,10],[60,61],[1,23],[4,54],[40,45]],[[9,13],[40,41],[6,27],[11,14],[8,14],[56,60],[18,20],[7,18],[45,46],[50,57],[37,51],[40,45],[30,31],[18,22],[10,11],[27,33],[27,40],[5,59],[25,31],[6,59],[15,59],[37,57],[30,61],[59,63],[34,39],[58,63],[49,52],[60,61],[57,59],[8,47],[12,15],[26,27]],[[23,46],[28,30],[51,53],[11,13],[27,46],[14,15],[8,34],[18,29],[40,43],[28,55],[52,54],[52,54],[40,47],[21,23],[44,55],[58,60],[20,41],[11,26],[7,55],[52,55],[30,44],[4,6],[18,41],[29,31],[24,30],[25,53],[48,49],[8,9],[10,41],[16,17],[14,35],[7,29]],[[58,60],[20,23],[28,31],[13,29],[34,36],[10,48],[8,15],[4,62],[50,52],[58,63],[16,37],[43,45],[35,36],[16,17],[0,33],[16,54],[8,60],[16,58],[37,38],[43,47],[42,45],[14,15],[16,18],[40,44],[13,17],[1,7],[57,61],[27,28],[32,43],[8,14],[35,38],[37,38]],[[16,21],[2,4],[42,44],[58,63],[5,45],[13,45],[8,10],[19,27],[50,51],[8,14],[26,30],[12,15],[32,38],[51,53],[58,61],[32,38],[57,61],[15,26],[3,5],[1,5],[58,61],[17,22],[24,30],[50,52],[59,61],[1,2],[47,54],[48,51],[31,55],[53,54],[4,28],[17,19]],[[50,54],[48,56],[11,51],[33,37],[0,5],[48,52],[49,55],[33,34],[51,55],[34,39],[6,20],[0,8],[0,7],[34,53],[50,53],[3,51],[28,31],[59,63],[11,15],[1,7],[21,34],[31,43],[19,22],[36,55],[7,18],[3,4],[14,40],[26,29],[25,26],[11,47],[4,61],[24,31]],[[10,15],[33,35],[53,62],[2,5],[13,15],[2,6],[2,7],[11,14],[10,14],[11,15],[1,7],[40,45],[11,26],[2,50],[45,46],[21,22],[17,18],[24,31],[24,29],[30,38],[42,45],[3,6],[48,55],[48,51],[18,22],[35,36],[6,23],[5,10],[50,52],[30,58],[53,54],[23,47]],[[50,51],[27,49],[23,44],[28,31],[6,14],[41,42],[49,53],[61,63],[42,45],[7,34],[15,46],[18,20],[57,61],[22,23],[28,31],[14,20],[25,27],[32,48],[26,29],[48,53],[37,38],[11,58],[29,36],[43,47],[2,5],[20,23],[12,15],[11,15],[2,5],[49,52],[47,48],[11,13]],[[27,56],[2,3],[34,46],[21,48],[38,39],[32,34],[11,14],[34,42],[9,12],[40,41],[38,62],[1,6],[50,59],[40,41],[11,51],[24,27],[8,39],[17,31],[28,29],[12,55],[50,52],[10,14],[9,13],[4,63],[40,44],[41,43],[51,55],[26,28],[17,18],[28,31],[40,43],[4,58]],[[3,34],[4,24],[24,28],[34,37],[24,29],[23,52],[0,10],[17,22],[53,61],[56,59],[38,39],[52,54],[15,26],[40,41],[7,54],[2,8],[11,15],[42,47],[30,37],[10,41],[51,55],[27,28],[9,15],[57,61],[58,62],[59,61],[40,42],[57,62],[46,59],[8,9],[2,7],[6,10]],[[17,21],[38,49],[56,63],[22,23],[16,22],[7,36],[56,62],[43,47],[10,15],[49,54],[26,31],[48,55],[20,38],[10,17],[56,57],[34,38],[17,48],[22,23],[41,44],[42,45],[16,23],[40,45],[11,12],[43,46],[11,39],[57,58],[53,54],[42,46],[3,30],[33,44],[3,6],[36,39]],[[40,42],[25,36],[56,59],[29,40],[58,63],[56,58],[6,13],[58,63],[57,58],[17,21],[12,48],[1,23],[11,18],[5,7],[12,16],[12,28],[43,51],[18,20],[0,21],[9,11],[10,11],[16,37],[0,5],[17,21],[18,21],[19,45],[8,28],[10,16],[35,38],[19,58],[32,53],[24,30]],[[40,47],[3,7],[57,59],[26,27],[51,54],[41,60],[16,20],[17,22],[31,33],[21,25],[8,47],[31,56],[27,29],[26,27],[32,39],[61,62],[22,23],[8,22],[19,63],[28,31],[2,4],[56,58],[23,61],[27,30],[20,23],[2,53],[48,53],[57,60],[56,62],[57,58],[58,59],[12,17]],[[33,37],[48,49],[25,28],[56,58],[0,22],[8,27],[11,15],[36,39],[1,9],[13,17],[14,30],[18,21],[25,27],[9,12],[32,34],[40,62],[18,20],[4,45],[52,53],[14,42],[45,50],[27,55],[16,21],[60,61],[25,28],[8,12],[44,53],[51,59],[49,52],[12,15],[3,15],[56,63]],[[11,23],[52,61],[46,47],[15,49],[2,4],[35,38],[10,12],[25,27],[28,31],[6,9],[8,18],[19,39],[50,52],[7,10],[38,51],[28,40],[50,57],[28,29],[30,56],[3,6],[2,11],[9,29],[49,51],[22,23],[10,12],[0,2],[60,62],[20,47],[58,62],[18,22],[4,58],[27,31]],[[35,54],[2,6],[45,49],[56,59],[1,5],[58,62],[32,38],[1,3],[12,58],[24,30],[51,55],[1,59],[11,13],[43,44],[62,63],[0,3],[5,6],[39,50],[20,23],[22,34],[50,56],[11,15],[3,7],[40,45],[5,6],[28,41],[58,61],[13,54],[8,10],[6,14],[45,46],[36,39]],[[42,43],[6,7],[59,63],[35,44],[49,54],[11,57],[14,61],[27,31],[8,9],[28,29],[39,52],[24,60],[41,46],[36,38],[2,14],[24,45],[24,31],[33,35],[26,29],[3,7],[14,15],[1,18],[2,3],[34,39],[24,25],[59,63],[49,54],[43,47],[32,38],[27,30],[28,31],[31,58]],[[50,54],[7,48],[49,53],[24,29],[39,47],[28,55],[36,47],[30,35],[37,52],[60,63],[46,61],[59,61],[25,41],[40,58],[59,60],[49,50],[2,55],[33,41],[25,26],[45,51],[12,48],[37,58],[60,62],[15,53],[11,12],[10,25],[41,43],[22,57],[24,27],[22,33],[1,4],[8,45]],[[26,56],[43,63],[32,47],[52,53],[25,51],[46,47],[49,53],[16,22],[18,22],[42,46],[3,57],[9,13],[9,37],[4,32],[27,31],[4,60],[34,37],[0,3],[7,48],[36,37],[1,6],[36,39],[42,44],[27,50],[35,52],[6,44],[17,40],[21,23],[16,22],[46,58],[15,44],[18,19]],[[44,45],[16,21],[0,2],[57,62],[11,18],[8,11],[8,12],[12,55],[20,62],[0,6],[9,14],[48,54],[18,22],[43,45],[10,14],[56,57],[37,39],[36,39],[44,54],[29,31],[5,48],[46,59],[36,38],[12,14],[20,22],[25,28],[22,42],[23,62],[11,14],[2,7],[52,54],[4,36]],[[38,52],[41,46],[30,31],[2,3],[12,14],[56,61],[2,5],[2,36],[9,59],[7,30],[33,36],[48,59],[48,55],[27,44],[1,3],[3,48],[24,48],[45,60],[12,14],[20,37],[49,55],[24,31],[49,54],[28,30],[61,62],[10,23],[29,30],[29,50],[0,14],[17,23],[0,2],[6,34]],[[48,51],[6,54],[32,47],[8,14],[12,59],[2,19],[33,36],[41,46],[10,44],[34,41],[9,12],[25,27],[2,53],[9,22],[37,39],[16,48],[16,18],[50,55],[4,7],[16,17],[14,39],[18,20],[5,31],[34,39],[17,52],[44,46],[2,33],[49,52],[8,11],[18,58],[21,51],[24,25]],[[12,25],[34,55],[35,39],[28,43],[16,49],[34,39],[1,8],[22,59],[25,26],[11,53],[49,53],[7,36],[24,31],[10,14],[36,38],[27,36],[54,55],[22,28],[51,55],[58,63],[56,61],[48,54],[41,44],[51,53],[35,39],[10,16],[3,5],[50,53],[9,15],[14,30],[28,31],[9,15]],[[17,20],[10,14],[6,24],[1,26],[51,53],[0,3],[16,17],[41,44],[17,51],[16,21],[9,13],[1,4],[22,44],[5,12],[48,55],[4,10],[56,62],[45,62],[0,1],[45,46],[5,47],[28,30],[17,34],[11,13],[52,53],[25,27],[16,42],[57,60],[10,54],[37,38],[0,1],[52,53]],[[60,62],[2,4],[15,22],[12,15],[40,45],[22,23],[32,59],[36,44],[58,59],[0,7],[61,63],[32,35],[4,6],[34,39],[45,46],[16,19],[5,7],[8,13],[9,33],[17,21],[14,30],[7,57],[26,31],[6,21],[37,48],[41,46],[3,60],[27,29],[1,2],[19,31],[2,35],[8,10]],[[4,12],[9,15],[13,36],[26,29],[0,50],[33,36],[51,52],[11,52],[1,52],[5,42],[10,12],[11,22],[16,18],[62,63],[52,53],[25,26],[28,40],[0,58],[56,59],[25,62],[25,48],[14,26],[27,63],[32,38],[24,57],[2,5],[24,31],[7,54],[41,60],[6,57],[1,7],[15,54]],[[39,61],[30,32],[3,7],[17,41],[41,43],[62,63],[44,46],[28,51],[51,53],[9,10],[9,59],[6,31],[19,21],[51,53],[26,30],[52,63],[27,29],[57,62],[22,38],[27,59],[12,13],[56,63],[8,9],[24,29],[23,53],[58,63],[33,36],[6,7],[56,58],[39,44],[19,60],[17,20]],[[50,51],[7,9],[28,57],[0,4],[35,39],[35,36],[0,7],[22,53],[56,63],[40,41],[36,38],[25,27],[58,63],[27,49],[51,53],[10,14],[34,46],[61,62],[6,25],[36,56],[7,25],[32,38],[28,29],[49,55],[50,54],[35,37],[16,21],[0,1],[25,62],[14,54],[60,61],[0,57]],[[41,43],[49,55],[24,27],[17,46],[44,46],[15,60],[0,3],[33,35],[2,7],[29,48],[8,11],[50,52],[8,55],[26,27],[4,14],[37,38],[0,31],[26,28],[34,57],[10,12],[40,46],[8,10],[33,39],[27,31],[8,47],[10,11],[0,5],[60,62],[26,28],[33,40],[27,46],[22,35]],[[53,61],[44,47],[28,57],[2,57],[16,46],[41,43],[59,63],[20,40],[32,39],[50,51],[2,52],[59,63],[25,27],[2,4],[20,23],[27,28],[32,62],[42,46],[0,5],[37,51],[3,43],[33,36],[27,29],[48,52],[44,45],[19,23],[59,62],[11,15],[10,18],[16,22],[54,55],[48,54]],[[25,28],[0,47],[32,37],[17,51],[28,41],[29,31],[18,19],[44,49],[27,28],[49,53],[25,27],[9,44],[31,42],[48,52],[48,52],[47,59],[36,39],[42,44],[21,22],[14,48],[19,45],[40,47],[34,37],[37,39],[18,55],[49,55],[57,63],[1,45],[3,6],[19,20],[58,60],[34,56]],[[36,59],[10,36],[33,50],[10,42],[2,3],[4,6],[25,28],[19,27],[48,52],[14,15],[32,48],[7,22],[4,41],[50,54],[49,51],[18,47],[40,41],[49,50],[36,61],[11,33],[24,31],[40,47],[32,33],[56,63],[40,47],[13,52],[10,47],[19,61],[49,55],[14,15],[50,54],[56,61]],[[16,46],[11,24],[34,38],[24,28],[40,47],[19,22],[22,23],[49,50],[58,61],[45,46],[41,42],[19,21],[1,5],[47,63],[21,58],[9,14],[44,45],[42,47],[49,52],[37,52],[40,46],[10,11],[40,61],[25,29],[40,46],[3,7],[12,15],[9,55],[21,29],[0,5],[3,4],[34,43]],[[50,53],[40,45],[44,45],[11,13],[41,43],[37,50],[51,55],[56,61],[13,15],[13,15],[26,31],[1,52],[37,39],[59,60],[23,51],[42,49],[15,23],[27,55],[59,60],[48,54],[43,47],[49,51],[35,37],[59,60],[34,38],[32,33],[3,7],[53,55],[60,61],[19,23],[10,12],[6,23]],[[4,14],[3,10],[10,14],[3,6],[41,42],[33,44],[41,42],[41,51],[19,40],[57,59],[25,26],[35,36],[0,54],[0,54],[41,42],[0,1],[23,47],[16,19],[17,60],[4,7],[17,22],[1,3],[52,61],[44,53],[8,11],[1,4],[25,36],[33,39],[22,43],[12,53],[40,41],[25,31]],[[35,42],[9,15],[33,34],[11,13],[33,39],[35,54],[35,57],[59,61],[34,35],[5,7],[3,30],[57,59],[23,58],[5,6],[2,57],[35,61],[15,50],[2,3],[32,33],[13,14],[2,28],[10,15],[2,6],[56,63],[4,5],[33,48],[9,30],[1,6],[4,6],[42,63],[1,4],[20,22]],[[43,55],[9,28],[27,31],[21,23],[1,40],[58,60],[13,15],[26,29],[13,23],[19,59],[10,51],[13,41],[16,22],[16,20],[1,36],[49,55],[25,29],[56,61],[41,45],[24,30],[20,62],[52,63],[4,6],[27,31],[19,20],[56,61],[24,60],[2,4],[31,36],[11,13],[8,15],[32,51]],[[27,44],[29,31],[17,21],[46,47],[34,35],[27,36],[32,35],[1,7],[16,17],[14,60],[7,29],[30,31],[39,46],[8,27],[59,63],[4,17],[29,61],[32,60],[11,32],[24,28],[32,44],[48,53],[24,31],[39,41],[56,63],[21,29],[19,47],[50,51],[26,31],[12,13],[58,61],[23,26]],[[15,44],[11,45],[14,26],[49,57],[17,20],[16,43],[35,60],[22,45],[10,24],[18,21],[38,39],[9,44],[2,7],[51,54],[14,17],[62,63],[25,31],[12,36],[16,20],[26,43],[52,59],[57,58],[27,55],[28,51],[9,13],[22,45],[0,4],[16,19],[16,21],[44,47],[1,61],[51,55]],[[1,29],[25,31],[10,12],[36,38],[2,49],[5,59],[8,30],[50,55],[48,50],[60,61],[2,40],[25,26],[48,61],[18,23],[30,31],[9,33],[27,38],[48,58],[48,55],[3,6],[10,49],[57,63],[20,23],[59,63],[59,63],[24,26],[42,51],[24,27],[17,40],[6,13],[12,13],[17,47]],[[42,46],[4,6],[48,50],[43,49],[49,50],[1,4],[19,21],[27,33],[43,45],[2,6],[51,52],[16,23],[42,43],[60,61],[41,47],[27,30],[8,38],[33,35],[27,31],[13,36],[4,29],[46,47],[2,27],[16,19],[20,23],[0,1],[61,63],[43,47],[1,17],[33,39],[31,63],[28,30]],[[21,42],[36,57],[6,18],[28,29],[19,44],[21,26],[40,51],[17,20],[49,55],[10,57],[17,19],[43,46],[2,5],[18,23],[0,53],[30,31],[49,59],[14,21],[28,48],[30,62],[35,36],[44,46],[45,46],[28,38],[56,59],[40,45],[2,5],[3,24],[10,13],[9,13],[14,54],[51,52]],[[33,36],[26,30],[42,48],[21,28],[34,35],[61,62],[14,56],[48,54],[32,34],[11,13],[42,43],[40,43],[36,39],[6,25],[40,47],[18,47],[46,47],[26,44],[4,5],[53,55],[53,55],[1,6],[23,30],[7,56],[25,27],[60,62],[15,26],[16,19],[2,6],[33,36],[42,46],[10,12]],[[60,61],[9,11],[25,27],[13,14],[9,12],[25,27],[49,55],[7,31],[23,24],[60,62],[41,45],[45,55],[25,56],[7,58],[18,22],[11,14],[42,62],[45,57],[20,23],[41,51],[56,57],[31,38],[27,30],[40,47],[4,24],[49,53],[37,39],[23,42],[29,47],[7,12],[25,30],[34,38]],[[33,41],[34,38],[25,30],[56,59],[0,2],[8,15],[54,63],[16,18],[24,30],[33,36],[42,61],[6,7],[2,6],[26,57],[61,62],[27,45],[6,19],[2,9],[8,14],[37,56],[37,38],[22,46],[41,59],[35,38],[27,28],[42,43],[56,59],[29,39],[29,32],[40,44],[39,40],[17,23]],[[0,22],[56,62],[5,27],[56,63],[10,13],[20,52],[51,53],[13,14],[26,40],[24,25],[0,7],[6,36],[20,55],[34,38],[10,15],[41,42],[6,36],[2,7],[12,22],[8,9],[9,32],[4,7],[58,62],[31,50],[8,10],[8,10],[0,2],[3,6],[24,29],[58,63],[12,18],[9,15]],[[23,25],[0,2],[31,36],[10,59],[24,26],[14,45],[19,28],[37,41],[62,63],[1,10],[10,46],[34,37],[6,15],[41,59],[11,15],[32,35],[54,59],[0,4],[41,44],[21,45],[57,59],[10,15],[23,43],[8,11],[0,2],[26,54],[22,62],[3,4],[45,46],[16,39],[19,22],[6,7]],[[48,52],[36,39],[10,11],[2,3],[43,57],[17,23],[46,62],[50,55],[59,60],[12,14],[4,5],[18,20],[7,44],[11,62],[1,4],[32,33],[22,41],[35,37],[16,18],[18,19],[22,48],[33,38],[16,23],[48,52],[29,33],[0,8],[45,46],[42,44],[25,31],[17,21],[48,62],[18,48]],[[37,45],[16,17],[19,20],[49,50],[3,4],[4,49],[43,47],[2,53],[19,35],[3,47],[21,45],[22,57],[1,7],[34,45],[4,60],[11,44],[0,1],[56,59],[24,58],[8,52],[58,62],[8,22],[0,7],[16,42],[12,15],[32,46],[36,39],[11,13],[10,13],[40,43],[49,50],[33,36]],[[24,61],[40,45],[41,52],[20,23],[35,39],[42,43],[57,60],[32,36],[30,35],[35,43],[10,11],[11,31],[34,47],[21,55],[29,31],[50,53],[49,55],[16,18],[25,43],[0,1],[26,31],[16,18],[5,7],[40,46],[23,25],[59,63],[34,38],[42,54],[24,50],[16,20],[58,61],[13,44]],[[26,31],[37,38],[1,3],[33,35],[2,4],[24,28],[24,33],[30,63],[6,49],[59,60],[17,19],[31,59],[17,22],[18,49],[49,51],[2,36],[32,39],[13,27],[23,51],[35,38],[55,59],[46,56],[30,31],[28,51],[51,54],[0,14],[29,56],[51,52],[27,60],[34,40],[33,36],[20,21]],[[44,45],[26,31],[56,58],[19,20],[12,13],[1,4],[14,25],[8,13],[36,37],[48,60],[45,62],[59,62],[33,36],[52,55],[11,60],[18,40],[49,51],[58,63],[41,42],[4,14],[2,49],[25,29],[53,55],[51,56],[56,60],[29,30],[17,20],[16,23],[32,34],[59,62],[15,60],[16,18]],[[49,51],[18,23],[28,29],[20,23],[15,39],[57,60],[19,39],[49,50],[58,62],[27,58],[22,50],[44,56],[10,12],[23,37],[25,26],[14,46],[10,15],[52,55],[32,38],[56,60],[58,61],[1,6],[11,26],[29,54],[2,39],[28,34],[42,43],[11,32],[26,31],[15,35],[12,15],[9,13]],[[38,39],[15,37],[4,6],[2,6],[17,23],[3,7],[58,62],[2,16],[23,39],[35,39],[9,13],[24,27],[2,3],[12,13],[20,28],[17,22],[11,39],[53,60],[11,49],[3,26],[29,54],[22,48],[45,47],[9,10],[1,7],[3,39],[5,26],[5,6],[58,62],[1,6],[19,21],[24,25]],[[42,48],[2,3],[26,31],[47,50],[2,51],[16,47],[5,7],[32,37],[59,63],[25,29],[32,35],[23,63],[6,41],[1,39],[40,45],[6,56],[36,63],[12,63],[56,58],[42,50],[36,37],[4,6],[1,32],[40,42],[10,14],[13,23],[10,51],[30,57],[6,46],[54,55],[22,23],[10,11]],[[57,58],[43,44],[24,25],[4,25],[15,46],[11,18],[24,26],[16,17],[40,62],[18,19],[20,21],[21,43],[29,30],[10,19],[18,21],[21,37],[59,60],[43,46],[41,45],[19,40],[5,7],[60,63],[44,47],[54,62],[18,23],[40,50],[13,15],[16,19],[56,57],[5,45],[1,4],[24,30]]]
CAP = 82
def setup_inputs(rng):
    return {"z": rng.standard_normal((N, CAP, D), dtype=np.float32)}
def reference(z):
    y = np.zeros((N, TOK, D), np.float64)
    fill = [0] * N
    for r in range(N):
        for t in range(TOK):
            for e in ROUTE[r][t]:
                if fill[e] < CAP:
                    y[r][t] += z[e][fill[e]]
                    fill[e] += 1
    return {"y": y.astype(z.dtype)}

@@ -1,0 +1,190 @@
+import concourse.bass as bass
+
+LAND_SLOTS = 64
+
+SCRATCH = {
+    "zs": ("dram", [82, 128, 4], "float32"),
+    "land": ("dram", [LAND_SLOTS, 128, 4], "float32"),
+    "out": ("dram", [32, 128, 4], "float32"),
+}
+SEMAPHORES = ["loaded", "read", "arr1", "arr2", "arrived", "stored"]
+
+PORT_CORES = (2, 3, 6, 7)
+CLASSES = {"co": 82.0, "ci": 72.0, "off": 44.0, "chi": 308.0, "mate": 84.0, "so": 132.0, "si": 130.0}
+POWER = 8
+PASSES = 6
+CACHE = {}
+
+
+def chip_of(c):
+    return c // 8
+
+
+def loads_of(topo, a, b):
+    out = [("co", a), ("ci", b)]
+    ca, cb = chip_of(a), chip_of(b)
+    if ca != cb:
+        d = topo.die(a)
+        out += [("off", a), ("chi", cb)]
+        if (ca ^ cb) & 1:
+            out.append(("mate", ca, d))
+            ca ^= 1
+        if ca != cb:
+            out += [("so", ca, d), ("si", cb, d)]
+    return out
+
+
+def ways(topo, r, e1, e2):
+    found = []
+    min_chip = len({chip_of(e1), chip_of(e2)} - {chip_of(r)})
+    min_host = 1 if ({topo.host(e1), topo.host(e2)} - {topo.host(r)}) else 0
+    for ch in sorted({chip_of(r), chip_of(e1), chip_of(e2)}):
+        for q in range(ch * 8, ch * 8 + 8):
+            if q == r or not topo.may_write(q, r):
+                continue
+            paths = []
+            for e in (e1, e2):
+                if e == q:
+                    paths.append([[]])
+                elif topo.may_write(e, q):
+                    paths.append([[(e, q)]])
+                else:
+                    paths.append([[(e, chip_of(e) * 8 + k), (chip_of(e) * 8 + k, q)] for k in PORT_CORES])
+            for pa in paths[0]:
+                for pb in paths[1]:
+                    w = pa + pb + [(q, r)]
+                    if sum(chip_of(a) != chip_of(b) for a, b in w) != min_chip:
+                        continue
+                    if sum(topo.host(a) != topo.host(b) for a, b in w) != min_host:
+                        continue
+                    found.append((q, pa, pb))
+    return found
+
+
+def plan(tables, cores, topo):
+    route, tok = tables["ROUTE"], tables["TOK"]
+    n = len(cores)
+    fill = [0] * n
+    tokens = []
+    for r in range(n):
+        for t in range(tok):
+            e1, e2 = route[r][t]
+            tokens.append((r, t, e1, fill[e1], e2, fill[e2]))
+            fill[e1] += 1
+            fill[e2] += 1
+
+    index, scale = {}, []
+    cand = []
+    for (r, t, e1, i1, e2, i2) in tokens:
+        cs = []
+        for (q, pa, pb) in ways(topo, cores[r], cores[e1], cores[e2]):
+            cnt = {}
+            for a, b in pa + pb + [(q, cores[r])]:
+                for k in loads_of(topo, a, b):
+                    if k not in index:
+                        index[k] = len(scale)
+                        scale.append(CLASSES[k[0]])
+                    cnt[index[k]] = cnt.get(index[k], 0) + 1
+            cs.append(((q, pa, pb), sorted(cnt.items())))
+        cand.append(cs)
+    tabs = {s: [(v / s) ** POWER for v in range(1024)] for s in set(scale)}
+    tab = [tabs[s] for s in scale]
+    load = [0] * len(scale)
+    choice = [-1] * len(tokens)
+    for sweep in range(PASSES):
+        changed = 0
+        for i, cs in enumerate(cand):
+            if choice[i] >= 0:
+                for k, m in cs[choice[i]][1]:
+                    load[k] -= m
+            best, best_j = None, 0
+            for j, (way, cnt) in enumerate(cs):
+                d = 0.0
+                for k, m in cnt:
+                    d += tab[k][load[k] + m] - tab[k][load[k]]
+                if best is None or d < best - 1e-12:
+                    best, best_j = d, j
+            changed += best_j != choice[i]
+            choice[i] = best_j
+            for k, m in cs[best_j][1]:
+                load[k] += m
+        if not changed:
+            break
+
+    prog = {c: {"rows": fill[k], "send": {1: [], 2: [], 3: []}, "arr": {1: 0, 2: 0}, "slots": 0} for k, c in enumerate(cores)}
+
+    def park(src_core, src, rnd, dst_core):
+        slot = prog[dst_core]["slots"]
+        prog[dst_core]["slots"] += 1
+        prog[src_core]["send"][rnd].append((dst_core, "land", slot, [src]))
+        prog[dst_core]["arr"][rnd] += 1
+        return ("land", slot)
+
+    for i, (r, t, e1, i1, e2, i2) in enumerate(tokens):
+        q, pa, pb = cand[i][choice[i]][0]
+        srcs, rnd = [], 1
+        for path, row in ((pa, i1), (pb, i2)):
+            src = ("zs", row)
+            for hop, (a, b) in enumerate(path):
+                src = park(a, src, hop + 1, b)
+            srcs.append(src)
+            rnd = max(rnd, len(path) + 1)
+        prog[q]["send"][rnd].append((cores[r], "out", t, srcs))
+    assert max(p["slots"] for p in prog.values()) <= LAND_SLOTS
+    return prog
+
+
+def calls_of(core, writes):
+    off = [w for w in writes if chip_of(w[0]) != chip_of(core)]
+    on = [w for w in writes if chip_of(w[0]) == chip_of(core)]
+    n_calls = max((len(off) + 7) // 8, (len(writes) + 15) // 16)
+    calls = []
+    for k in range(n_calls):
+        left = n_calls - k
+        n_off = (len(off) + left - 1) // left
+        n_on = min(16 - n_off, (len(on) + left - 1) // left)
+        calls.append(off[:n_off] + on[:n_on])
+        off, on = off[n_off:], on[n_on:]
+    assert not off and not on
+    return calls
+
+
+def rank_program(g, core, T, topo):
+    if T.rank_of(core) is None:
+        return
+    if "plan" not in CACHE:
+        CACHE["plan"] = plan(T.tables, list(T.cores), topo)
+    me = CACHE["plan"][core]
+    buf = {"zs": T.zs, "land": T.land, "out": T.out}
+    sem_of = {("land", 1): T.sem.arr1, ("land", 2): T.sem.arr2}
+
+    rows = me["rows"]
+    g.dma_start(T.zs[0:rows], T.z[0:rows, :]).then_inc(T.sem.loaded, 16)
+    g.wait_ge(T.sem.loaded, 16)
+
+    sent = 0
+    for rnd in (1, 2, 3):
+        if rnd > 1 and me["arr"][rnd - 1]:
+            g.wait_ge(sem_of[("land", rnd - 1)], me["arr"][rnd - 1])
+        for call in calls_of(core, me["send"][rnd]):
+            transfers = []
+            for eng, (dst, name, slot, srcs) in enumerate(call):
+                rid, pid = topo.addr(dst, core)
+                sem = T.sem.arrived if name == "out" else sem_of[(name, rnd)]
+                aps = [buf[s][k] for s, k in srcs]
+                if len(aps) == 1:
+                    transfers.append(bass.RemoteDMATransfer(
+                        dst_ids=[bass.DstId(rid=rid, pnc=pid)], dma_engine_mask=1 << eng, remote_sem=sem,
+                        src=aps[0], dst=buf[name][slot], alu_op=0))
+                else:
+                    transfers.append(bass.RemoteDMATransfer(
+                        dst_ids=[bass.DstId(rid=rid, pnc=pid)], dma_engine_mask=1 << eng, remote_sem=sem,
+                        srcs=aps, dsts=[buf[name][slot]], alu_op=1))
+            g.remote_dma_fused(transfers, local_sem=T.sem.read)
+            sent += len(call)
+
+    g.wait_ge(T.sem.arrived, T.tables["TOK"])
+    g.dma_start(T.y[:, :], T.out[:]).then_inc(T.sem.stored, 16)
+    g.wait_ge(T.sem.stored, 16)
+    if sent:
+        g.wait_ge(T.sem.read, sent)

@@ -1,18 +1,18 @@
 import concourse.bass as bass
 
-LAND_SLOTS = 64
+LAND_SLOTS = 48
 
 SCRATCH = {
     "zs": ("dram", [82, 128, 4], "float32"),
     "land": ("dram", [LAND_SLOTS, 128, 4], "float32"),
     "out": ("dram", [32, 128, 4], "float32"),
 }
-SEMAPHORES = ["loaded", "read", "arr1", "arr2", "arrived", "stored"]
+SEMAPHORES = ["loaded", "read", "near", "far", "arrived", "stored"]
 
 PORT_CORES = (2, 3, 6, 7)
-CLASSES = {"co": 82.0, "ci": 72.0, "off": 44.0, "chi": 308.0, "mate": 84.0, "so": 132.0, "si": 130.0}
-POWER = 8
-PASSES = 6
+SCALES = {"co": 88.0, "ci": 78.0, "off": 50.0, "chi": 312.0, "mate": 83.0, "so": 134.0, "si": 130.0}
+POWERS = (4, 16, 64, 128)
+PASSES = 4
 CACHE = {}
 
 
@@ -61,6 +61,117 @@ def ways(topo, r, e1, e2):
     return found
 
 
+def choose_ways(topo, triples):
+    index, scale, cand = {}, [], []
+    for (r, e1, e2) in triples:
+        cs = []
+        for (q, pa, pb) in ways(topo, r, e1, e2):
+            cnt = {}
+            for a, b in pa + pb + [(q, r)]:
+                for k in loads_of(topo, a, b):
+                    if k not in index:
+                        index[k] = len(scale)
+                        scale.append(SCALES[k[0]])
+                    cnt[index[k]] = cnt.get(index[k], 0) + 1
+            cs.append(((q, pa, pb), sorted(cnt.items())))
+        cand.append(cs)
+    load = [0] * len(scale)
+    choice = [-1] * len(cand)
+    for power in POWERS:
+        tabs = {s: [(v / s) ** power for v in range(1024)] for s in set(scale)}
+        tab = [tabs[s] for s in scale]
+        for sweep in range(PASSES):
+            changed = 0
+            for i, cs in enumerate(cand):
+                if choice[i] >= 0:
+                    for k, m in cs[choice[i]][1]:
+                        load[k] -= m
+                best, best_j = None, 0
+                for j, (way, cnt) in enumerate(cs):
+                    d = 0.0
+                    for k, m in cnt:
+                        d += tab[k][load[k] + m] - tab[k][load[k]]
+                    if best is None or d < best - 1e-12:
+                        best, best_j = d, j
+                changed += best_j != choice[i]
+                choice[i] = best_j
+                for k, m in cs[best_j][1]:
+                    load[k] += m
+            if not changed:
+                break
+    return [cand[i][choice[i]][0] for i in range(len(cand))]
+
+
+ONLY1, ONE_OR_TWO, ONLY2, TWO_OR_THREE, ONLY3 = range(5)
+
+
+def fill_rounds(count, calls):
+    carry, early = [0, 0], []
+    for k in range(3):
+        on = count[2 * k][0] + carry[0]
+        off = count[2 * k][1] + carry[1]
+        if off > 8 * calls[k] or on + off > 16 * calls[k]:
+            return None
+        if k < 2:
+            free = count[2 * k + 1]
+            x_off = min(free[1], 8 * calls[k] - off, 16 * calls[k] - on - off)
+            x_on = min(free[0], 16 * calls[k] - on - off - x_off)
+            carry = [free[0] - x_on, free[1] - x_off]
+            early.append([x_on, x_off])
+    return early
+
+
+def fewest_calls(count):
+    total = 0
+    while True:
+        for c1 in range(total, -1, -1):
+            for c2 in range(total - c1, -1, -1):
+                calls = (c1, c2, total - c1 - c2)
+                early = fill_rounds(count, calls)
+                if early is not None:
+                    return total, calls, early
+        total += 1
+
+
+def schedule(cores, owners, chosen):
+    def is_off(a, b):
+        return int(chip_of(a) != chip_of(b))
+
+    late = []
+    for (q, pa, pb) in chosen:
+        late.append(any(len(p) == 2 or (len(p) == 1 and is_off(*p[0])) for p in (pa, pb)))
+    count = {c: [[0, 0] for k in range(5)] for c in cores}
+
+    def book(i, sign):
+        q, pa, pb = chosen[i]
+        for p in (pa, pb):
+            if len(p) == 2:
+                count[p[0][0]][ONLY1][0] += sign
+                count[p[1][0]][ONLY2][is_off(*p[1])] += sign
+            elif len(p) == 1:
+                count[p[0][0]][ONE_OR_TWO if late[i] else ONLY1][is_off(*p[0])] += sign
+        count[q][ONLY3 if late[i] else TWO_OR_THREE][is_off(q, owners[i])] += sign
+
+    for i in range(len(chosen)):
+        book(i, 1)
+    goal = max(max((sum(k[1] for k in n) + 7) // 8, (sum(k[0] + k[1] for k in n) + 15) // 16) for n in count.values())
+    for c in cores:
+        for i, (q, pa, pb) in enumerate(chosen):
+            if fewest_calls(count[c])[0] <= goal:
+                break
+            if late[i] or not any(len(p) == 1 and p[0][0] == c for p in (pa, pb)):
+                continue
+            before = fewest_calls(count[q])[0]
+            book(i, -1)
+            late[i] = True
+            book(i, 1)
+            if fewest_calls(count[q])[0] > max(goal, before):
+                book(i, -1)
+                late[i] = False
+                book(i, 1)
+    return late
+
+
 def plan(tables, cores, topo):
     route, tok = tables["ROUTE"], tables["TOK"]
     n = len(cores)
@@ -72,65 +183,43 @@ def plan(tables, cores, topo):
             tokens.append((r, t, e1, fill[e1], e2, fill[e2]))
             fill[e1] += 1
             fill[e2] += 1
+    chosen = choose_ways(topo, [(cores[r], cores[e1], cores[e2]) for (r, t, e1, i1, e2, i2) in tokens])
+    late = schedule(cores, [cores[tk[0]] for tk in tokens], chosen)
 
-    index, scale = {}, []
-    cand = []
-    for (r, t, e1, i1, e2, i2) in tokens:
-        cs = []
-        for (q, pa, pb) in ways(topo, cores[r], cores[e1], cores[e2]):
-            cnt = {}
-            for a, b in pa + pb + [(q, cores[r])]:
-                for k in loads_of(topo, a, b):
-                    if k not in index:
-                        index[k] = len(scale)
-                        scale.append(CLASSES[k[0]])
-                    cnt[index[k]] = cnt.get(index[k], 0) + 1
-            cs.append(((q, pa, pb), sorted(cnt.items())))
-        cand.append(cs)
-    tabs = {s: [(v / s) ** POWER for v in range(1024)] for s in set(scale)}
-    tab = [tabs[s] for s in scale]
-    load = [0] * len(scale)
-    choice = [-1] * len(tokens)
-    for sweep in range(PASSES):
-        changed = 0
-        for i, cs in enumerate(cand):
-            if choice[i] >= 0:
-                for k, m in cs[choice[i]][1]:
-                    load[k] -= m
-            best, best_j = None, 0
-            for j, (way, cnt) in enumerate(cs):
-                d = 0.0
-                for k, m in cnt:
-                    d += tab[k][load[k] + m] - tab[k][load[k]]
-                if best is None or d < best - 1e-12:
-                    best, best_j = d, j
-            changed += best_j != choice[i]
-            choice[i] = best_j
-            for k, m in cs[best_j][1]:
-                load[k] += m
-        if not changed:
-            break
+    prog = {c: {"rows": fill[k], "cls": [[[], []] for j in range(5)], "near": 0, "far": 0, "slots": 0}
+            for k, c in enumerate(cores)}
 
-    prog = {c: {"rows": fill[k], "send": {1: [], 2: [], 3: []}, "arr": {1: 0, 2: 0}, "slots": 0} for k, c in enumerate(cores)}
-
-    def park(src_core, src, rnd, dst_core):
-        slot = prog[dst_core]["slots"]
-        prog[dst_core]["slots"] += 1
-        prog[src_core]["send"][rnd].append((dst_core, "land", slot, [src]))
-        prog[dst_core]["arr"][rnd] += 1
+    def park(a, src, cls, b, sem):
+        slot = prog[b]["slots"]
+        prog[b]["slots"] += 1
+        prog[b][sem] += 1
+        prog[a]["cls"][cls][int(chip_of(a) != chip_of(b))].append((b, "land", slot, sem, [src]))
         return ("land", slot)
 
     for i, (r, t, e1, i1, e2, i2) in enumerate(tokens):
-        q, pa, pb = cand[i][choice[i]][0]
-        srcs, rnd = [], 1
+        q, pa, pb = chosen[i]
+        srcs = []
         for path, row in ((pa, i1), (pb, i2)):
             src = ("zs", row)
-            for hop, (a, b) in enumerate(path):
-                src = park(a, src, hop + 1, b)
+            if len(path) == 2:
+                src = park(path[0][0], src, ONLY1, path[0][1], "near")
+                src = park(path[1][0], src, ONLY2, path[1][1], "far")
+            elif len(path) == 1:
+                src = park(path[0][0], src, ONE_OR_TWO if late[i] else ONLY1, path[0][1], "far" if late[i] else "near")
             srcs.append(src)
-            rnd = max(rnd, len(path) + 1)
-        prog[q]["send"][rnd].append((cores[r], "out", t, srcs))
+        prog[q]["cls"][ONLY3 if late[i] else TWO_OR_THREE][int(chip_of(q) != chip_of(cores[r]))].append(
+            (cores[r], "out", t, "arrived", srcs))
     assert max(p["slots"] for p in prog.values()) <= LAND_SLOTS
+
+    for p in prog.values():
+        cls = p["cls"]
+        total, calls, early = fewest_calls([[len(k[0]), len(k[1])] for k in cls])
+        rounds = [cls[ONLY1][0] + cls[ONLY1][1], cls[ONLY2][0] + cls[ONLY2][1], cls[ONLY3][0] + cls[ONLY3][1]]
+        for k, free in enumerate((cls[ONE_OR_TWO], cls[TWO_OR_THREE])):
+            for side in (0, 1):
+                rounds[k] += free[side][:early[k][side]]
+                rounds[k + 1] += free[side][early[k][side]:]
+        p["rounds"] = rounds
     return prog
 
 
@@ -156,29 +245,30 @@ def rank_program(g, core, T, topo):
         CACHE["plan"] = plan(T.tables, list(T.cores), topo)
     me = CACHE["plan"][core]
     buf = {"zs": T.zs, "land": T.land, "out": T.out}
-    sem_of = {("land", 1): T.sem.arr1, ("land", 2): T.sem.arr2}
+    sem = {"near": T.sem.near, "far": T.sem.far, "arrived": T.sem.arrived}
 
     rows = me["rows"]
     g.dma_start(T.zs[0:rows], T.z[0:rows, :]).then_inc(T.sem.loaded, 16)
     g.wait_ge(T.sem.loaded, 16)
 
     sent = 0
-    for rnd in (1, 2, 3):
-        if rnd > 1 and me["arr"][rnd - 1]:
-            g.wait_ge(sem_of[("land", rnd - 1)], me["arr"][rnd - 1])
-        for call in calls_of(core, me["send"][rnd]):
+    for k, writes in enumerate(me["rounds"]):
+        if k == 1 and me["near"]:
+            g.wait_ge(T.sem.near, me["near"])
+        if k == 2 and me["far"]:
+            g.wait_ge(T.sem.far, me["far"])
+        for call in calls_of(core, writes):
             transfers = []
-            for eng, (dst, name, slot, srcs) in enumerate(call):
+            for eng, (dst, name, slot, sem_name, srcs) in enumerate(call):
                 rid, pid = topo.addr(dst, core)
-                sem = T.sem.arrived if name == "out" else sem_of[(name, rnd)]
-                aps = [buf[s][k] for s, k in srcs]
+                aps = [buf[s][j] for s, j in srcs]
                 if len(aps) == 1:
                     transfers.append(bass.RemoteDMATransfer(
-                        dst_ids=[bass.DstId(rid=rid, pnc=pid)], dma_engine_mask=1 << eng, remote_sem=sem,
+                        dst_ids=[bass.DstId(rid=rid, pnc=pid)], dma_engine_mask=1 << eng, remote_sem=sem[sem_name],
                         src=aps[0], dst=buf[name][slot], alu_op=0))
                 else:
                     transfers.append(bass.RemoteDMATransfer(
-                        dst_ids=[bass.DstId(rid=rid, pnc=pid)], dma_engine_mask=1 << eng, remote_sem=sem,
+                        dst_ids=[bass.DstId(rid=rid, pnc=pid)], dma_engine_mask=1 << eng, remote_sem=sem[sem_name],
                         srcs=aps, dsts=[buf[name][slot]], alu_op=1))
             g.remote_dma_fused(transfers, local_sem=T.sem.read)
             sent += len(call)

@@ -1,6 +1,6 @@
 import concourse.bass as bass
 
-LAND_SLOTS = 48
+LAND_SLOTS = 46
 
 SCRATCH = {
     "zs": ("dram", [82, 128, 4], "float32"),
@@ -10,7 +10,7 @@ SCRATCH = {
 SEMAPHORES = ["loaded", "read", "near", "far", "arrived", "stored"]
 
 PORT_CORES = (2, 3, 6, 7)
-SCALES = {"co": 88.0, "ci": 78.0, "off": 50.0, "chi": 312.0, "mate": 83.0, "so": 134.0, "si": 130.0}
+SCALES = {"co": 88.0, "ci": 78.0, "off": 55.0, "chi": 310.0, "mate": 83.0, "so": 134.0, "si": 130.0}
 POWERS = (4, 16, 64, 128)
 PASSES = 4
 CACHE = {}
@@ -61,6 +61,10 @@ def ways(topo, r, e1, e2):
     return found
 
 
+def size_of(way):
+    return len(way[1]) + len(way[2]) + 1
+
+
 def choose_ways(topo, triples):
     index, scale, cand = {}, [], []
     for (r, e1, e2) in triples:
@@ -99,6 +103,27 @@ def choose_ways(topo, triples):
                     load[k] += m
             if not changed:
                 break
+
+    names = sorted(index, key=index.get)
+    top = {}
+    for k, key in enumerate(names):
+        top[key[0]] = max(top.get(key[0], 0), load[k])
+    cap = [top[key[0]] for key in names]
+    for sweep in range(PASSES):
+        changed = 0
+        for i, cs in enumerate(cand):
+            for k, m in cs[choice[i]][1]:
+                load[k] -= m
+            best_j = choice[i]
+            for j, (way, cnt) in enumerate(cs):
+                if size_of(way) < size_of(cs[best_j][0]) and all(load[k] + m <= cap[k] for k, m in cnt):
+                    best_j = j
+            changed += best_j != choice[i]
+            choice[i] = best_j
+            for k, m in cs[best_j][1]:
+                load[k] += m
+        if not changed:
+            break
     return [cand[i][choice[i]][0] for i in range(len(cand))]
 
 

import concourse.bass as bass

LAND_SLOTS = 46

SCRATCH = {
    "zs": ("dram", [82, 128, 4], "float32"),
    "land": ("dram", [LAND_SLOTS, 128, 4], "float32"),
    "out": ("dram", [32, 128, 4], "float32"),
}
SEMAPHORES = ["loaded", "read", "near", "far", "arrived", "stored"]

PORT_CORES = (2, 3, 6, 7)
SCALES = {"co": 88.0, "ci": 78.0, "off": 55.0, "chi": 310.0, "mate": 83.0, "so": 134.0, "si": 130.0}
POWERS = (4, 16, 64, 128)
PASSES = 4
CACHE = {}


def chip_of(c):
    return c // 8


def loads_of(topo, a, b):
    out = [("co", a), ("ci", b)]
    ca, cb = chip_of(a), chip_of(b)
    if ca != cb:
        d = topo.die(a)
        out += [("off", a), ("chi", cb)]
        if (ca ^ cb) & 1:
            out.append(("mate", ca, d))
            ca ^= 1
        if ca != cb:
            out += [("so", ca, d), ("si", cb, d)]
    return out


def ways(topo, r, e1, e2):
    found = []
    min_chip = len({chip_of(e1), chip_of(e2)} - {chip_of(r)})
    min_host = 1 if ({topo.host(e1), topo.host(e2)} - {topo.host(r)}) else 0
    for ch in sorted({chip_of(r), chip_of(e1), chip_of(e2)}):
        for q in range(ch * 8, ch * 8 + 8):
            if q == r or not topo.may_write(q, r):
                continue
            paths = []
            for e in (e1, e2):
                if e == q:
                    paths.append([[]])
                elif topo.may_write(e, q):
                    paths.append([[(e, q)]])
                else:
                    paths.append([[(e, chip_of(e) * 8 + k), (chip_of(e) * 8 + k, q)] for k in PORT_CORES])
            for pa in paths[0]:
                for pb in paths[1]:
                    w = pa + pb + [(q, r)]
                    if sum(chip_of(a) != chip_of(b) for a, b in w) != min_chip:
                        continue
                    if sum(topo.host(a) != topo.host(b) for a, b in w) != min_host:
                        continue
                    found.append((q, pa, pb))
    return found


def size_of(way):
    return len(way[1]) + len(way[2]) + 1


def choose_ways(topo, triples):
    index, scale, cand = {}, [], []
    for (r, e1, e2) in triples:
        cs = []
        for (q, pa, pb) in ways(topo, r, e1, e2):
            cnt = {}
            for a, b in pa + pb + [(q, r)]:
                for k in loads_of(topo, a, b):
                    if k not in index:
                        index[k] = len(scale)
                        scale.append(SCALES[k[0]])
                    cnt[index[k]] = cnt.get(index[k], 0) + 1
            cs.append(((q, pa, pb), sorted(cnt.items())))
        cand.append(cs)
    load = [0] * len(scale)
    choice = [-1] * len(cand)
    for power in POWERS:
        tabs = {s: [(v / s) ** power for v in range(1024)] for s in set(scale)}
        tab = [tabs[s] for s in scale]
        for sweep in range(PASSES):
            changed = 0
            for i, cs in enumerate(cand):
                if choice[i] >= 0:
                    for k, m in cs[choice[i]][1]:
                        load[k] -= m
                best, best_j = None, 0
                for j, (way, cnt) in enumerate(cs):
                    d = 0.0
                    for k, m in cnt:
                        d += tab[k][load[k] + m] - tab[k][load[k]]
                    if best is None or d < best - 1e-12:
                        best, best_j = d, j
                changed += best_j != choice[i]
                choice[i] = best_j
                for k, m in cs[best_j][1]:
                    load[k] += m
            if not changed:
                break

    names = sorted(index, key=index.get)
    top = {}
    for k, key in enumerate(names):
        top[key[0]] = max(top.get(key[0], 0), load[k])
    cap = [top[key[0]] for key in names]
    for sweep in range(PASSES):
        changed = 0
        for i, cs in enumerate(cand):
            for k, m in cs[choice[i]][1]:
                load[k] -= m
            best_j = choice[i]
            for j, (way, cnt) in enumerate(cs):
                if size_of(way) < size_of(cs[best_j][0]) and all(load[k] + m <= cap[k] for k, m in cnt):
                    best_j = j
            changed += best_j != choice[i]
            choice[i] = best_j
            for k, m in cs[best_j][1]:
                load[k] += m
        if not changed:
            break
    return [cand[i][choice[i]][0] for i in range(len(cand))]


ONLY1, ONE_OR_TWO, ONLY2, TWO_OR_THREE, ONLY3 = range(5)


def fill_rounds(count, calls):
    carry, early = [0, 0], []
    for k in range(3):
        on = count[2 * k][0] + carry[0]
        off = count[2 * k][1] + carry[1]
        if off > 8 * calls[k] or on + off > 16 * calls[k]:
            return None
        if k < 2:
            free = count[2 * k + 1]
            x_off = min(free[1], 8 * calls[k] - off, 16 * calls[k] - on - off)
            x_on = min(free[0], 16 * calls[k] - on - off - x_off)
            carry = [free[0] - x_on, free[1] - x_off]
            early.append([x_on, x_off])
    return early


def fewest_calls(count):
    total = 0
    while True:
        for c1 in range(total, -1, -1):
            for c2 in range(total - c1, -1, -1):
                calls = (c1, c2, total - c1 - c2)
                early = fill_rounds(count, calls)
                if early is not None:
                    return total, calls, early
        total += 1


def schedule(cores, owners, chosen):
    def is_off(a, b):
        return int(chip_of(a) != chip_of(b))

    late = []
    for (q, pa, pb) in chosen:
        late.append(any(len(p) == 2 or (len(p) == 1 and is_off(*p[0])) for p in (pa, pb)))
    count = {c: [[0, 0] for k in range(5)] for c in cores}

    def book(i, sign):
        q, pa, pb = chosen[i]
        for p in (pa, pb):
            if len(p) == 2:
                count[p[0][0]][ONLY1][0] += sign
                count[p[1][0]][ONLY2][is_off(*p[1])] += sign
            elif len(p) == 1:
                count[p[0][0]][ONE_OR_TWO if late[i] else ONLY1][is_off(*p[0])] += sign
        count[q][ONLY3 if late[i] else TWO_OR_THREE][is_off(q, owners[i])] += sign

    for i in range(len(chosen)):
        book(i, 1)
    goal = max(max((sum(k[1] for k in n) + 7) // 8, (sum(k[0] + k[1] for k in n) + 15) // 16) for n in count.values())
    for c in cores:
        for i, (q, pa, pb) in enumerate(chosen):
            if fewest_calls(count[c])[0] <= goal:
                break
            if late[i] or not any(len(p) == 1 and p[0][0] == c for p in (pa, pb)):
                continue
            before = fewest_calls(count[q])[0]
            book(i, -1)
            late[i] = True
            book(i, 1)
            if fewest_calls(count[q])[0] > max(goal, before):
                book(i, -1)
                late[i] = False
                book(i, 1)
    return late


def plan(tables, cores, topo):
    route, tok = tables["ROUTE"], tables["TOK"]
    n = len(cores)
    fill = [0] * n
    tokens = []
    for r in range(n):
        for t in range(tok):
            e1, e2 = route[r][t]
            tokens.append((r, t, e1, fill[e1], e2, fill[e2]))
            fill[e1] += 1
            fill[e2] += 1
    chosen = choose_ways(topo, [(cores[r], cores[e1], cores[e2]) for (r, t, e1, i1, e2, i2) in tokens])
    late = schedule(cores, [cores[tk[0]] for tk in tokens], chosen)

    prog = {c: {"rows": fill[k], "cls": [[[], []] for j in range(5)], "near": 0, "far": 0, "slots": 0}
            for k, c in enumerate(cores)}

    def park(a, src, cls, b, sem):
        slot = prog[b]["slots"]
        prog[b]["slots"] += 1
        prog[b][sem] += 1
        prog[a]["cls"][cls][int(chip_of(a) != chip_of(b))].append((b, "land", slot, sem, [src]))
        return ("land", slot)

    for i, (r, t, e1, i1, e2, i2) in enumerate(tokens):
        q, pa, pb = chosen[i]
        srcs = []
        for path, row in ((pa, i1), (pb, i2)):
            src = ("zs", row)
            if len(path) == 2:
                src = park(path[0][0], src, ONLY1, path[0][1], "near")
                src = park(path[1][0], src, ONLY2, path[1][1], "far")
            elif len(path) == 1:
                src = park(path[0][0], src, ONE_OR_TWO if late[i] else ONLY1, path[0][1], "far" if late[i] else "near")
            srcs.append(src)
        prog[q]["cls"][ONLY3 if late[i] else TWO_OR_THREE][int(chip_of(q) != chip_of(cores[r]))].append(
            (cores[r], "out", t, "arrived", srcs))
    assert max(p["slots"] for p in prog.values()) <= LAND_SLOTS

    for p in prog.values():
        cls = p["cls"]
        total, calls, early = fewest_calls([[len(k[0]), len(k[1])] for k in cls])
        rounds = [cls[ONLY1][0] + cls[ONLY1][1], cls[ONLY2][0] + cls[ONLY2][1], cls[ONLY3][0] + cls[ONLY3][1]]
        for k, free in enumerate((cls[ONE_OR_TWO], cls[TWO_OR_THREE])):
            for side in (0, 1):
                rounds[k] += free[side][:early[k][side]]
                rounds[k + 1] += free[side][early[k][side]:]
        p["rounds"] = rounds
    return prog


def calls_of(core, writes):
    off = [w for w in writes if chip_of(w[0]) != chip_of(core)]
    on = [w for w in writes if chip_of(w[0]) == chip_of(core)]
    n_calls = max((len(off) + 7) // 8, (len(writes) + 15) // 16)
    calls = []
    for k in range(n_calls):
        left = n_calls - k
        n_off = (len(off) + left - 1) // left
        n_on = min(16 - n_off, (len(on) + left - 1) // left)
        calls.append(off[:n_off] + on[:n_on])
        off, on = off[n_off:], on[n_on:]
    assert not off and not on
    return calls


def rank_program(g, core, T, topo):
    if T.rank_of(core) is None:
        return
    if "plan" not in CACHE:
        CACHE["plan"] = plan(T.tables, list(T.cores), topo)
    me = CACHE["plan"][core]
    buf = {"zs": T.zs, "land": T.land, "out": T.out}
    sem = {"near": T.sem.near, "far": T.sem.far, "arrived": T.sem.arrived}

    rows = me["rows"]
    g.dma_start(T.zs[0:rows], T.z[0:rows, :]).then_inc(T.sem.loaded, 16)
    g.wait_ge(T.sem.loaded, 16)

    sent = 0
    for k, writes in enumerate(me["rounds"]):
        if k == 1 and me["near"]:
            g.wait_ge(T.sem.near, me["near"])
        if k == 2 and me["far"]:
            g.wait_ge(T.sem.far, me["far"])
        for call in calls_of(core, writes):
            transfers = []
            for eng, (dst, name, slot, sem_name, srcs) in enumerate(call):
                rid, pid = topo.addr(dst, core)
                aps = [buf[s][j] for s, j in srcs]
                if len(aps) == 1:
                    transfers.append(bass.RemoteDMATransfer(
                        dst_ids=[bass.DstId(rid=rid, pnc=pid)], dma_engine_mask=1 << eng, remote_sem=sem[sem_name],
                        src=aps[0], dst=buf[name][slot], alu_op=0))
                else:
                    transfers.append(bass.RemoteDMATransfer(
                        dst_ids=[bass.DstId(rid=rid, pnc=pid)], dma_engine_mask=1 << eng, remote_sem=sem[sem_name],
                        srcs=aps, dsts=[buf[name][slot]], alu_op=1))
            g.remote_dma_fused(transfers, local_sem=T.sem.read)
            sent += len(call)

    g.wait_ge(T.sem.arrived, T.tables["TOK"])
    g.dma_start(T.y[:, :], T.out[:]).then_inc(T.sem.stored, 16)
    g.wait_ge(T.sem.stored, 16)
    if sent:
        g.wait_ge(T.sem.read, sent)
